import numpy as np
import ml_dtypes


def mxq(x, axis, fmt="e4m3"):
    dtype, down = {"e4m3": (ml_dtypes.float8_e4m3fn, 7), "e5m2": (ml_dtypes.float8_e5m2, 14)}[fmt]
    v = np.moveaxis(np.asarray(x, np.float32).astype(ml_dtypes.bfloat16).astype(np.float64), axis, -1)
    blocks = v.reshape(v.shape[:-1] + (-1, 32))
    amax = np.abs(blocks).max(-1, keepdims=True)
    byte = np.maximum(np.where(amax > 0, np.frexp(amax)[1] - 1 + 127, 0) - down, 1)
    scale = np.exp2(byte - 127.0)
    codes = (blocks / scale).astype(np.float32).astype(dtype).astype(np.float64)
    return np.moveaxis((codes * scale).reshape(v.shape), -1, axis)


WIDE = False


def mx_kscale(k):
    if not WIDE:
        return np.ones(k)
    levels = np.array([10, -10, 5, -5, 0])
    if k % 512:
        return np.exp2(np.random.permutation(np.resize(levels, k // 32))).repeat(32)
    a = np.empty((k // 512, 16))
    for p in range(k // 512):
        a[p, :8] = np.random.permutation(np.resize(levels, 8))
        for g in range(8):
            far = levels[np.abs(levels - a[p, g]) >= 10]
            a[p, g + 8] = far[np.random.randint(len(far))]
    return np.exp2(a.ravel()).repeat(32)


def f64(x):
    return np.asarray(x).astype(np.float64)


def striped(idx):
    return np.tile(idx.reshape(-1, 16).T, (8, 1)).astype(np.uint16)


def unstriped(offs):
    return offs[:16].T.reshape(-1).astype(np.int64)


def silu(v):
    return v / (1.0 + np.exp(-np.maximum(v, -700.0)))


K, T, E, C, H, N = 512, 1024, 4, 256, 512, 128


def by_expert(wq, xq):
    return np.concatenate([wq[e].T @ xq[:, e * C:(e + 1) * C] for e in range(E)], axis=1)


def setup_inputs():
    n = np.random.standard_normal
    s = mx_kscale(K)[:, None]
    u = mx_kscale(H)
    return {
        "xT": (n((K, T)) * s).astype(np.float32),
        "w1": (n((E, K, H)) / np.sqrt(K) / s[None] * u[None, None, :]).astype(np.float32),
        "w2": (n((E, H, N)) / np.sqrt(H) / u[None, :, None]).astype(np.float32),
        "gate": np.tile(np.random.uniform(0.2, 1.0, E * C), (N, 1)).astype(np.float32),
        "offs": striped(np.random.permutation(T)[:E * C]),
    }


def reference(xT, w1, w2, gate, offs):
    idx = unstriped(offs)
    xq = mxq(f64(xT)[:, idx], 0, "e4m3")
    h = silu(by_expert(mxq(f64(w1), 1, "e4m3"), xq))
    y = by_expert(mxq(f64(w2), 1, "e4m3"), mxq(h, 0, "e4m3"))
    out = np.zeros((N, T))
    out[:, idx] = f64(gate) * y
    return out

@@ -1,0 +1,178 @@
+from contextlib import ExitStack
+
+import concourse.mybir as mybir
+
+K, T, E, C, H, N = 512, 1024, 4, 256, 512, 128
+FLOPS = 2 * E * C * (K * H + H * N)
+
+F32 = mybir.dt.float32
+BF16 = mybir.dt.bfloat16
+U32 = mybir.dt.uint32
+U16 = mybir.dt.uint16
+U8 = mybir.dt.uint8
+FP8X4 = mybir.dt.float8_e4m3fn_x4
+MULT = mybir.AluOpType.mult
+ADD = mybir.AluOpType.add
+SILU = mybir.ActivationFunctionType.Silu
+
+P = 128
+PACK = 4
+GROUP = 512
+HALF = 128
+
+W1_PARTS = (("s", 0, 64), ("g", 64, 128))
+W2_PARTS = (("v", 0, 4),)
+LOADS = "offs p0 p1 p2 p3 w10 w11 w12 w13 w2 gate"
+TEXT = "g:0.0 g:0.1 g:0.2 g:0.3 qx:0 g:1.0 g:1.1 g:1.2 g:1.3 qx:1 wi:0.0 wi:0.1 qw:0 wi:1.0 wi:1.1 qw:1 wi:2.0 wi:2.1 qw:2 wi:3.0 wi:3.1 qw:3 mm1:0.0 mm1:0.1 mm1:1.0 mm1:1.1 mm1:2.0 mm1:2.1 si:0.0 si:0.1 si:1.0 si:1.1 w2i:0 qw2:0 qh:0 qh:1 mm1:3.0 mm1:3.1 mm2:0 yc:0 si:2.0 si:2.1 qh:2 mm2:1 yc:1 si:3.0 si:3.1 qh:3 mm2:2 yc:2 mm2:3 yc:3 sc:0 sc:1 sc:2 sc:3"
+
+
+def move(nc, engine, out, in_):
+    if engine == "v":
+        nc.vector.tensor_copy(out=out, in_=in_)
+    elif engine == "s":
+        nc.scalar.copy(out=out, in_=in_)
+    else:
+        nc.gpsimd.tensor_scalar(out, in_, 1.0, 0.0, MULT, ADD)
+
+
+def tile_routed_moe_kernel(tc, xT, w1, w2, gate, offs, out):
+    nc = tc.nc
+    with ExitStack() as ctx:
+        lists = ctx.enter_context(tc.tile_pool(name="lists", bufs=1))
+        keep = ctx.enter_context(tc.tile_pool(name="keep", bufs=1))
+        xrot = ctx.enter_context(tc.tile_pool(name="xrot", bufs=1))
+        psum1 = ctx.enter_context(tc.psum_pool(name="psum1", bufs=6))
+        psum2 = ctx.enter_context(tc.psum_pool(name="psum2", bufs=2))
+
+        offsets = lists.tile([P, T // 16], U16, name="offsets")
+        x_view = xT.rearrange("(p t) n -> p t n", t=PACK)
+        x_raw = keep.tile([P, PACK, T], F32, name="x_raw")
+        w1_raw = [keep.tile([P, PACK, H], F32, name="w1raw%d" % e, align_bytes=64) for e in range(E - 1)]
+        w1_raw.append(keep.tile([P, PACK, H], F32, name="w1raw_last", tag="slot_a", align_bytes=64))
+        w2_raw = keep.tile([P, E, PACK, N], F32, name="w2raw")
+        gate_sb = keep.tile([P, E * C], F32, name="gate_sb")
+        for what in LOADS.split():
+            if what == "offs":
+                nc.sync.dma_start(offsets[:], offs)
+            elif what == "w2":
+                nc.sync.dma_start(
+                    w2_raw[:].rearrange("p e j n -> p e (j n)"),
+                    w2.rearrange("e (p j) n -> p e (j n)", j=PACK),
+                )
+            elif what == "gate":
+                nc.sync.dma_start(gate_sb[:], gate)
+            elif what.startswith("p"):
+                t = int(what[1:])
+                nc.sync.dma_start(x_raw[:, t, :], x_view[:, t, :])
+            else:
+                e = int(what[2:])
+                nc.sync.dma_start(w1_raw[e][:], w1[e].rearrange("(p j) c -> p j c", j=PACK))
+
+        warm_in = keep.tile([P, 1], F32, name="warm_in")
+        warm_out = keep.tile([P, 1], F32, name="warm_out")
+        nc.vector.memset(warm_in[:], 0.0)
+        nc.scalar.activation(out=warm_out[:], in_=warm_in[:], func=SILU)
+
+        window = keep.tile([P, T], F32, name="window")
+        w1b = [keep.tile([P, PACK * H], BF16, name="w1b%d" % e, align_bytes=64) for e in range(E)]
+        w1c = [keep.tile([P, H], U32, name="w1c%d" % e, align_bytes=64) for e in range(E)]
+        w1s = [keep.tile([P, H], U8, name="w1s%d" % e, align_bytes=64) for e in range(E)]
+        xc = [keep.tile([P, GROUP], U32, name="xc%d" % g, align_bytes=64) for g in range(2)]
+        xs = [keep.tile([P, GROUP], U8, name="xs%d" % g, align_bytes=64) for g in range(2)]
+        hc = keep.tile([P, E * C], U32, name="hc", align_bytes=64)
+        y = [keep.tile([P, C], F32, name="y%d" % e) for e in range(E)]
+        w2b = keep.tile([P, E, N, PACK], BF16, name="w2b", tag="slot_b", align_bytes=64)
+        w2c = keep.tile([P, E * N], U32, name="w2c", align_bytes=64)
+        w2s = keep.tile([P, E * N], U8, name="w2s", align_bytes=64)
+        xb, banks, accs, late = {}, {}, {}, {}
+
+        for step in TEXT.split():
+            kind, arg = step.split(":")
+            a = [int(v) for v in arg.split(".")]
+            if kind == "g":
+                g, t = a
+                if g not in xb:
+                    xb[g] = xrot.tile([P, GROUP, PACK], BF16, name="xb", align_bytes=64)
+                cols = slice(g * GROUP // 16, (g + 1) * GROUP // 16)
+                nc.vector.tensor_copy(xb[g][:, :, t], x_raw[:, t, :].indirect(offsets[:, cols]))
+            elif kind == "qx":
+                g = a[0]
+                nc.vector.quantize_mx(
+                    out=xc[g][:].bitcast(FP8X4), scales=xs[g][:], in_=xb[g][:].rearrange("p n t -> p (n t)")
+                )
+            elif kind == "wi":
+                e, i = a
+                engine, m0, m1 = W1_PARTS[i]
+                dst = w1b[e][:].rearrange("p (t m j) -> p m t j", t=PACK, j=PACK)
+                src = w1_raw[e][:].rearrange("p j (m t) -> p m t j", t=PACK)
+                move(nc, engine, dst[:, m0:m1, :, :], src[:, m0:m1, :, :])
+            elif kind == "qw":
+                e = a[0]
+                nc.vector.quantize_mx(out=w1c[e][:].bitcast(FP8X4), scales=w1s[e][:], in_=w1b[e][:])
+            elif kind == "mm1":
+                e, half = a
+                g, c0 = (e * C) // GROUP, (e * C) % GROUP + half * HALF
+                banks[(e, half)] = psum1.tile([P, PACK, HALF], F32, name="bank")
+                for t in range(PACK):
+                    chans = slice(t * P, (t + 1) * P)
+                    nc.tensor.matmul_mx(
+                        out=banks[(e, half)][:, t, :],
+                        lhsT=w1c[e][:, chans].bitcast(FP8X4),
+                        lhsT_scale=w1s[e][:, chans],
+                        rhs=xc[g][:, c0 : c0 + HALF].bitcast(FP8X4),
+                        rhs_scale=xs[g][:, c0 : c0 + HALF],
+                        start=True,
+                        stop=True,
+                    )
+            elif kind == "si":
+                e, half = a
+                if "hb" not in late:
+                    late["hb"] = keep.tile([P, E * C, PACK], BF16, name="hb", tag="slot_a", align_bytes=64)
+                nc.scalar.activation(
+                    out=late["hb"][:, e * C + half * HALF : e * C + (half + 1) * HALF, :],
+                    in_=banks[(e, half)][:].rearrange("p t n -> p n t"),
+                    func=SILU,
+                )
+            elif kind == "qh":
+                e = a[0]
+                if "hs" not in late:
+                    late["hs"] = keep.tile([P, E * C], U8, name="hs", tag="slot_b", align_bytes=64)
+                slots = slice(e * C, (e + 1) * C)
+                nc.vector.quantize_mx(
+                    out=hc[:, slots].bitcast(FP8X4),
+                    scales=late["hs"][:, slots],
+                    in_=late["hb"][:, slots, :].rearrange("p n t -> p (n t)"),
+                )
+            elif kind == "w2i":
+                engine, e0, e1 = W2_PARTS[a[0]]
+                move(nc, engine, w2b[:, e0:e1, :, :], w2_raw[:, e0:e1, :, :].rearrange("p e j n -> p e n j"))
+            elif kind == "qw2":
+                nc.vector.quantize_mx(
+                    out=w2c[:].bitcast(FP8X4), scales=w2s[:], in_=w2b[:].rearrange("p e n j -> p (e n j)")
+                )
+            elif kind == "mm2":
+                e = a[0]
+                accs[e] = psum2.tile([P, C], F32, name="acc")
+                feats = slice(e * N, (e + 1) * N)
+                nc.tensor.matmul_mx(
+                    out=accs[e][:],
+                    lhsT=w2c[:, feats].bitcast(FP8X4),
+                    lhsT_scale=w2s[:, feats],
+                    rhs=hc[:, e * C : (e + 1) * C].bitcast(FP8X4),
+                    rhs_scale=late["hs"][:, e * C : (e + 1) * C],
+                    start=True,
+                    stop=True,
+                )
+            elif kind == "yc":
+                e = a[0]
+                nc.scalar.copy(out=y[e][:], in_=accs[e][:])
+            else:
+                e = a[0]
+                nc.vector.tensor_tensor(
+                    window[:].indirect(offsets[:, e * C // 16 : (e + 1) * C // 16]),
+                    y[e][:],
+                    gate_sb[:, e * C : (e + 1) * C],
+                    MULT,
+                )
+
+        nc.sync.dma_start(out, window[:])

@@ -14,6 +14,7 @@ FP8X4 = mybir.dt.float8_e4m3fn_x4
 MULT = mybir.AluOpType.mult
 ADD = mybir.AluOpType.add
 SILU = mybir.ActivationFunctionType.Silu
+COPY = mybir.ActivationFunctionType.Copy
 
 P = 128
 PACK = 4
@@ -23,7 +24,7 @@ HALF = 128
 W1_PARTS = (("s", 0, 64), ("g", 64, 128))
 W2_PARTS = (("v", 0, 4),)
 LOADS = "offs p0 p1 p2 p3 w10 w11 w12 w13 w2 gate"
-TEXT = "g:0.0 g:0.1 g:0.2 g:0.3 qx:0 g:1.0 g:1.1 g:1.2 g:1.3 qx:1 wi:0.0 wi:0.1 qw:0 wi:1.0 wi:1.1 qw:1 wi:2.0 wi:2.1 qw:2 wi:3.0 wi:3.1 qw:3 mm1:0.0 mm1:0.1 mm1:1.0 mm1:1.1 mm1:2.0 mm1:2.1 si:0.0 si:0.1 si:1.0 si:1.1 w2i:0 qw2:0 qh:0 qh:1 mm1:3.0 mm1:3.1 mm2:0 yc:0 si:2.0 si:2.1 qh:2 mm2:1 yc:1 si:3.0 si:3.1 qh:3 mm2:2 yc:2 mm2:3 yc:3 sc:0 sc:1 sc:2 sc:3"
+TEXT = "cast:0 cast:1 cast:2 cast:3 g:0.0 g:0.1 g:0.2 g:0.3 qx:0 fg:0 fg:1 fg:2 fg:3 g:2.0 g:2.1 g:2.2 g:2.3 qx:2 qx:3 wi:0.0 wi:0.1 qw:0 wi:1.0 wi:1.1 qw:1 wi:2.0 wi:2.1 qw:2 wi:3.0 wi:3.1 qw:3 mm1:0.0 mm1:0.1 mm1:1.0 mm1:1.1 mm1:2.0 mm1:2.1 si:0.0 si:0.1 si:1.0 si:1.1 w2i:0 qw2:0 qh:0 qh:1 mm1:3.0 mm1:3.1 mm2:0 yc:0 si:2.0 si:2.1 qh:2 mm2:1 yc:1 si:3.0 si:3.1 qh:3 mm2:2 yc:2 mm2:3 yc:3 sc:0 sc:1 sc:2 sc:3"
 
 
 def move(nc, engine, out, in_):
@@ -47,6 +48,7 @@ def tile_routed_moe_kernel(tc, xT, w1, w2, gate, offs, out):
         offsets = lists.tile([P, T // 16], U16, name="offsets")
         x_view = xT.rearrange("(p t) n -> p t n", t=PACK)
         x_raw = keep.tile([P, PACK, T], F32, name="x_raw")
+        x_bf = keep.tile([P, PACK, T], BF16, name="x_bf")
         w1_raw = [keep.tile([P, PACK, H], F32, name="w1raw%d" % e, align_bytes=64) for e in range(E - 1)]
         w1_raw.append(keep.tile([P, PACK, H], F32, name="w1raw_last", tag="slot_a", align_bytes=64))
         w2_raw = keep.tile([P, E, PACK, N], F32, name="w2raw")
@@ -77,14 +79,16 @@ def tile_routed_moe_kernel(tc, xT, w1, w2, gate, offs, out):
         w1b = [keep.tile([P, PACK * H], BF16, name="w1b%d" % e, align_bytes=64) for e in range(E)]
         w1c = [keep.tile([P, H], U32, name="w1c%d" % e, align_bytes=64) for e in range(E)]
         w1s = [keep.tile([P, H], U8, name="w1s%d" % e, align_bytes=64) for e in range(E)]
-        xc = [keep.tile([P, GROUP], U32, name="xc%d" % g, align_bytes=64) for g in range(2)]
-        xs = [keep.tile([P, GROUP], U8, name="xs%d" % g, align_bytes=64) for g in range(2)]
+        span = {0: (0, 2 * C), 2: (2 * C, C), 3: (3 * C, C)}
+        xc = {g: keep.tile([P, span[g][1]], U32, name="xc%d" % g, align_bytes=64) for g in span}
+        xs = {g: keep.tile([P, span[g][1]], U8, name="xs%d" % g, align_bytes=64) for g in span}
         hc = keep.tile([P, E * C], U32, name="hc", align_bytes=64)
         y = [keep.tile([P, C], F32, name="y%d" % e) for e in range(E)]
         w2b = keep.tile([P, E, N, PACK], BF16, name="w2b", tag="slot_b", align_bytes=64)
         w2c = keep.tile([P, E * N], U32, name="w2c", align_bytes=64)
         w2s = keep.tile([P, E * N], U8, name="w2s", align_bytes=64)
         xb, banks, accs, late = {}, {}, {}, {}
+        xb[3] = keep.tile([P, C, PACK], BF16, name="xb_s", align_bytes=64)
 
         for step in TEXT.split():
             kind, arg = step.split(":")
@@ -92,9 +96,16 @@ def tile_routed_moe_kernel(tc, xT, w1, w2, gate, offs, out):
             if kind == "g":
                 g, t = a
                 if g not in xb:
-                    xb[g] = xrot.tile([P, GROUP, PACK], BF16, name="xb", align_bytes=64)
-                cols = slice(g * GROUP // 16, (g + 1) * GROUP // 16)
+                    xb[g] = xrot.tile([P, span[g][1], PACK], BF16, name="xb", align_bytes=64)
+                cols = slice(span[g][0] // 16, (span[g][0] + span[g][1]) // 16)
                 nc.vector.tensor_copy(xb[g][:, :, t], x_raw[:, t, :].indirect(offsets[:, cols]))
+            elif kind == "cast":
+                t = a[0]
+                nc.scalar.copy(out=x_bf[:, t, :], in_=x_raw[:, t, :])
+            elif kind == "fg":
+                t = a[0]
+                cols = slice(span[3][0] // 16, (span[3][0] + span[3][1]) // 16)
+                nc.scalar.activation(out=xb[3][:, :, t], in_=x_bf[:, t, :].indirect(offsets[:, cols]), func=COPY)
             elif kind == "qx":
                 g = a[0]
                 nc.vector.quantize_mx(
@@ -111,7 +122,8 @@ def tile_routed_moe_kernel(tc, xT, w1, w2, gate, offs, out):
                 nc.vector.quantize_mx(out=w1c[e][:].bitcast(FP8X4), scales=w1s[e][:], in_=w1b[e][:])
             elif kind == "mm1":
                 e, half = a
-                g, c0 = (e * C) // GROUP, (e * C) % GROUP + half * HALF
+                g = 0 if e < 2 else e
+                c0 = e * C - span[g][0] + half * HALF
                 banks[(e, half)] = psum1.tile([P, PACK, HALF], F32, name="bank")
                 for t in range(PACK):
                     chans = slice(t * P, (t + 1) * P)

@@ -21,10 +21,10 @@ PACK = 4
 GROUP = 512
 HALF = 128
 
-W1_PARTS = (("s", 0, 64), ("g", 64, 128))
+W1_PARTS = ((("v", 0, 128),), (("s", 0, 128),), (("s", 0, 96), ("v", 96, 128)), (("v", 0, 128),))
 W2_PARTS = (("v", 0, 4),)
 LOADS = "offs p0 p1 p2 p3 w10 w11 w12 w13 w2 gate"
-TEXT = "cast:0 cast:1 cast:2 cast:3 g:0.0 g:0.1 g:0.2 g:0.3 qx:0 fg:0 fg:1 fg:2 fg:3 g:2.0 g:2.1 g:2.2 g:2.3 qx:2 qx:3 wi:0.0 wi:0.1 qw:0 wi:1.0 wi:1.1 qw:1 wi:2.0 wi:2.1 qw:2 wi:3.0 wi:3.1 qw:3 mm1:0.0 mm1:0.1 mm1:1.0 mm1:1.1 mm1:2.0 mm1:2.1 si:0.0 si:0.1 si:1.0 si:1.1 w2i:0 qw2:0 qh:0 qh:1 mm1:3.0 mm1:3.1 mm2:0 yc:0 si:2.0 si:2.1 qh:2 mm2:1 yc:1 si:3.0 si:3.1 qh:3 mm2:2 yc:2 mm2:3 yc:3 sc:0 sc:1 sc:2 sc:3"
+TEXT = "cast:0 cast:1 cast:2 cast:3 g:0.0 g:0.1 g:0.2 g:0.3 qx:0 fg:0 fg:1 fg:2 fg:3 g:2.0 g:2.1 g:2.2 g:2.3 qx:2 qx:3 wi:0.0 qw:0 wi:1.0 qw:1 wi:2.0 wi:2.1 qw:2 wi:3.0 qw:3 mm1:0.0 mm1:0.1 mm1:1.0 mm1:1.1 mm1:2.0 mm1:2.1 si:0.0 si:0.1 si:1.0 si:1.1 w2i:0 qw2:0 qh:0 qh:1 mm1:3.0 mm1:3.1 mm2:0 yc:0 si:2.0 si:2.1 qh:2 mm2:1 yc:1 si:3.0 si:3.1 qh:3 mm2:2 yc:2 mm2:3 yc:3 sc:0 sc:1 sc:2 sc:3"
 
 
 def move(nc, engine, out, in_):
@@ -49,8 +49,10 @@ def tile_routed_moe_kernel(tc, xT, w1, w2, gate, offs, out):
         x_view = xT.rearrange("(p t) n -> p t n", t=PACK)
         x_raw = keep.tile([P, PACK, T], F32, name="x_raw")
         x_bf = keep.tile([P, PACK, T], BF16, name="x_bf")
-        w1_raw = [keep.tile([P, PACK, H], F32, name="w1raw%d" % e, align_bytes=64) for e in range(E - 1)]
-        w1_raw.append(keep.tile([P, PACK, H], F32, name="w1raw_last", tag="slot_a", align_bytes=64))
+        w1_raw = [
+            keep.tile([P, PACK, H], F32, name="w1raw%d" % e, tag=("slot_a" if e == 2 else "w1raw%d" % e), align_bytes=64)
+            for e in range(E)
+        ]
         w2_raw = keep.tile([P, E, PACK, N], F32, name="w2raw")
         gate_sb = keep.tile([P, E * C], F32, name="gate_sb")
         for what in LOADS.split():
@@ -113,7 +115,7 @@ def tile_routed_moe_kernel(tc, xT, w1, w2, gate, offs, out):
                 )
             elif kind == "wi":
                 e, i = a
-                engine, m0, m1 = W1_PARTS[i]
+                engine, m0, m1 = W1_PARTS[e][i]
                 dst = w1b[e][:].rearrange("p (t m j) -> p m t j", t=PACK, j=PACK)
                 src = w1_raw[e][:].rearrange("p j (m t) -> p m t j", t=PACK)
                 move(nc, engine, dst[:, m0:m1, :, :], src[:, m0:m1, :, :])

@@ -21,10 +21,10 @@ PACK = 4
 GROUP = 512
 HALF = 128
 
-W1_PARTS = ((("v", 0, 128),), (("s", 0, 128),), (("s", 0, 96), ("v", 96, 128)), (("v", 0, 128),))
+W1_PARTS = ((("s", 0, 32), ("g", 32, 128)), (("s", 0, 32), ("g", 32, 128)), (("s", 0, 64), ("g", 64, 128)), (("g", 0, 64), ("v", 64, 128)))
 W2_PARTS = (("v", 0, 4),)
 LOADS = "offs p0 p1 p2 p3 w10 w11 w12 w13 w2 gate"
-TEXT = "cast:0 cast:1 cast:2 cast:3 g:0.0 g:0.1 g:0.2 g:0.3 qx:0 fg:0 fg:1 fg:2 fg:3 g:2.0 g:2.1 g:2.2 g:2.3 qx:2 qx:3 wi:0.0 qw:0 wi:1.0 qw:1 wi:2.0 wi:2.1 qw:2 wi:3.0 qw:3 mm1:0.0 mm1:0.1 mm1:1.0 mm1:1.1 mm1:2.0 mm1:2.1 si:0.0 si:0.1 si:1.0 si:1.1 w2i:0 qw2:0 qh:0 qh:1 mm1:3.0 mm1:3.1 mm2:0 yc:0 si:2.0 si:2.1 qh:2 mm2:1 yc:1 si:3.0 si:3.1 qh:3 mm2:2 yc:2 mm2:3 yc:3 sc:0 sc:1 sc:2 sc:3"
+TEXT = "cast:0 cast:1 cast:2 cast:3 g:0.0 g:0.1 g:0.2 g:0.3 qx:0 fg:0 fg:1 fg:2 fg:3 g:2.0 g:2.1 g:2.2 g:2.3 qx:2 qx:3 wi:0.0 wi:0.1 qw:0 wi:1.0 wi:1.1 qw:1 wi:2.0 wi:2.1 qw:2 wi:3.0 wi:3.1 qw:3 mm1:0.0 mm1:0.1 mm1:1.0 mm1:1.1 mm1:2.0 mm1:2.1 si:0.0 si:0.1 si:1.0 si:1.1 w2i:0 qw2:0 qh:0 qh:1 mm1:3.0 mm1:3.1 mm2:0 yc:0 si:2.0 si:2.1 qh:2 mm2:1 yc:1 si:3.0 si:3.1 qh:3 mm2:2 yc:2 mm2:3 yc:3 sc:0 sc:1 sc:2 sc:3"
 
 
 def move(nc, engine, out, in_):

@@ -18,22 +18,14 @@ COPY = mybir.ActivationFunctionType.Copy
 
 P = 128
 PACK = 4
-GROUP = 512
 HALF = 128
-
-W1_PARTS = ((("s", 0, 32), ("g", 32, 128)), (("s", 0, 32), ("g", 32, 128)), (("s", 0, 64), ("g", 64, 128)), (("g", 0, 64), ("v", 64, 128)))
-W2_PARTS = (("v", 0, 4),)
-LOADS = "offs p0 p1 p2 p3 w10 w11 w12 w13 w2 gate"
-TEXT = "cast:0 cast:1 cast:2 cast:3 g:0.0 g:0.1 g:0.2 g:0.3 qx:0 fg:0 fg:1 fg:2 fg:3 g:2.0 g:2.1 g:2.2 g:2.3 qx:2 qx:3 wi:0.0 wi:0.1 qw:0 wi:1.0 wi:1.1 qw:1 wi:2.0 wi:2.1 qw:2 wi:3.0 wi:3.1 qw:3 mm1:0.0 mm1:0.1 mm1:1.0 mm1:1.1 mm1:2.0 mm1:2.1 si:0.0 si:0.1 si:1.0 si:1.1 w2i:0 qw2:0 qh:0 qh:1 mm1:3.0 mm1:3.1 mm2:0 yc:0 si:2.0 si:2.1 qh:2 mm2:1 yc:1 si:3.0 si:3.1 qh:3 mm2:2 yc:2 mm2:3 yc:3 sc:0 sc:1 sc:2 sc:3"
-
-
-def move(nc, engine, out, in_):
-    if engine == "v":
-        nc.vector.tensor_copy(out=out, in_=in_)
-    elif engine == "s":
-        nc.scalar.copy(out=out, in_=in_)
-    else:
-        nc.gpsimd.tensor_scalar(out, in_, 1.0, 0.0, MULT, ADD)
+V_SLOTS = 3 * C
+W1_PARTS = (
+    (("g", 0, 32), ("v", 32, 128)),
+    (("s", 0, 64), ("g", 64, 128)),
+    (("s", 0, 64), ("g", 64, 128)),
+    (("s", 0, 96), ("g", 96, 128)),
+)
 
 
 def tile_routed_moe_kernel(tc, xT, w1, w2, gate, offs, out):
@@ -41,152 +33,160 @@ def tile_routed_moe_kernel(tc, xT, w1, w2, gate, offs, out):
     with ExitStack() as ctx:
         lists = ctx.enter_context(tc.tile_pool(name="lists", bufs=1))
         keep = ctx.enter_context(tc.tile_pool(name="keep", bufs=1))
-        xrot = ctx.enter_context(tc.tile_pool(name="xrot", bufs=1))
         psum1 = ctx.enter_context(tc.psum_pool(name="psum1", bufs=6))
         psum2 = ctx.enter_context(tc.psum_pool(name="psum2", bufs=2))
 
         offsets = lists.tile([P, T // 16], U16, name="offsets")
+        nc.sync.dma_start(offsets[:], offs)
         x_view = xT.rearrange("(p t) n -> p t n", t=PACK)
         x_raw = keep.tile([P, PACK, T], F32, name="x_raw")
-        x_bf = keep.tile([P, PACK, T], BF16, name="x_bf")
+        for t in range(PACK):
+            nc.sync.dma_start(x_raw[:, t, :], x_view[:, t, :])
         w1_raw = [
-            keep.tile([P, PACK, H], F32, name="w1raw%d" % e, tag=("slot_a" if e == 2 else "w1raw%d" % e), align_bytes=64)
+            keep.tile([P, PACK, H], F32, name="w1raw%d" % e, tag=("slot_a" if e == E - 1 else "w1raw%d" % e), align_bytes=64)
             for e in range(E)
         ]
+        for e in range(E):
+            nc.sync.dma_start(w1_raw[e][:], w1[e].rearrange("(p j) c -> p j c", j=PACK))
         w2_raw = keep.tile([P, E, PACK, N], F32, name="w2raw")
+        nc.sync.dma_start(
+            w2_raw[:].rearrange("p e j n -> p e (j n)"), w2.rearrange("e (p j) n -> p e (j n)", j=PACK)
+        )
         gate_sb = keep.tile([P, E * C], F32, name="gate_sb")
-        for what in LOADS.split():
-            if what == "offs":
-                nc.sync.dma_start(offsets[:], offs)
-            elif what == "w2":
-                nc.sync.dma_start(
-                    w2_raw[:].rearrange("p e j n -> p e (j n)"),
-                    w2.rearrange("e (p j) n -> p e (j n)", j=PACK),
-                )
-            elif what == "gate":
-                nc.sync.dma_start(gate_sb[:], gate)
-            elif what.startswith("p"):
-                t = int(what[1:])
-                nc.sync.dma_start(x_raw[:, t, :], x_view[:, t, :])
-            else:
-                e = int(what[2:])
-                nc.sync.dma_start(w1_raw[e][:], w1[e].rearrange("(p j) c -> p j c", j=PACK))
+        nc.sync.dma_start(gate_sb[:], gate)
 
         warm_in = keep.tile([P, 1], F32, name="warm_in")
         warm_out = keep.tile([P, 1], F32, name="warm_out")
         nc.vector.memset(warm_in[:], 0.0)
         nc.scalar.activation(out=warm_out[:], in_=warm_in[:], func=SILU)
 
-        window = keep.tile([P, T], F32, name="window")
-        w1b = [keep.tile([P, PACK * H], BF16, name="w1b%d" % e, align_bytes=64) for e in range(E)]
-        w1c = [keep.tile([P, H], U32, name="w1c%d" % e, align_bytes=64) for e in range(E)]
-        w1s = [keep.tile([P, H], U8, name="w1s%d" % e, align_bytes=64) for e in range(E)]
-        span = {0: (0, 2 * C), 2: (2 * C, C), 3: (3 * C, C)}
-        xc = {g: keep.tile([P, span[g][1]], U32, name="xc%d" % g, align_bytes=64) for g in span}
-        xs = {g: keep.tile([P, span[g][1]], U8, name="xs%d" % g, align_bytes=64) for g in span}
-        hc = keep.tile([P, E * C], U32, name="hc", align_bytes=64)
-        y = [keep.tile([P, C], F32, name="y%d" % e) for e in range(E)]
-        w2b = keep.tile([P, E, N, PACK], BF16, name="w2b", tag="slot_b", align_bytes=64)
-        w2c = keep.tile([P, E * N], U32, name="w2c", align_bytes=64)
-        w2s = keep.tile([P, E * N], U8, name="w2s", align_bytes=64)
-        xb, banks, accs, late = {}, {}, {}, {}
-        xb[3] = keep.tile([P, C, PACK], BF16, name="xb_s", align_bytes=64)
+        x_bf = keep.tile([P, PACK, T], BF16, name="x_bf")
+        xb = keep.tile([P, E * C, PACK], BF16, name="xb", align_bytes=64)
+        xc = keep.tile([P, E * C], U32, name="xc", align_bytes=64)
+        xs = keep.tile([P, E * C], U8, name="xs", align_bytes=64)
+        for t in range(PACK):
+            nc.scalar.copy(out=x_bf[:, t, :], in_=x_raw[:, t, :])
+        for t in range(PACK):
+            nc.vector.tensor_copy(xb[:, 0:V_SLOTS, t], x_raw[:, t, :].indirect(offsets[:, 0 : V_SLOTS // 16]))
+        for t in range(PACK):
+            nc.scalar.activation(
+                out=xb[:, V_SLOTS : E * C, t],
+                in_=x_bf[:, t, :].indirect(offsets[:, V_SLOTS // 16 : E * C // 16]),
+                func=COPY,
+            )
+        nc.vector.quantize_mx(out=xc[:].bitcast(FP8X4), scales=xs[:], in_=xb[:].rearrange("p n t -> p (n t)"))
 
-        for step in TEXT.split():
-            kind, arg = step.split(":")
-            a = [int(v) for v in arg.split(".")]
-            if kind == "g":
-                g, t = a
-                if g not in xb:
-                    xb[g] = xrot.tile([P, span[g][1], PACK], BF16, name="xb", align_bytes=64)
-                cols = slice(span[g][0] // 16, (span[g][0] + span[g][1]) // 16)
-                nc.vector.tensor_copy(xb[g][:, :, t], x_raw[:, t, :].indirect(offsets[:, cols]))
-            elif kind == "cast":
-                t = a[0]
-                nc.scalar.copy(out=x_bf[:, t, :], in_=x_raw[:, t, :])
-            elif kind == "fg":
-                t = a[0]
-                cols = slice(span[3][0] // 16, (span[3][0] + span[3][1]) // 16)
-                nc.scalar.activation(out=xb[3][:, :, t], in_=x_bf[:, t, :].indirect(offsets[:, cols]), func=COPY)
-            elif kind == "qx":
-                g = a[0]
-                nc.vector.quantize_mx(
-                    out=xc[g][:].bitcast(FP8X4), scales=xs[g][:], in_=xb[g][:].rearrange("p n t -> p (n t)")
-                )
-            elif kind == "wi":
-                e, i = a
-                engine, m0, m1 = W1_PARTS[e][i]
-                dst = w1b[e][:].rearrange("p (t m j) -> p m t j", t=PACK, j=PACK)
-                src = w1_raw[e][:].rearrange("p j (m t) -> p m t j", t=PACK)
-                move(nc, engine, dst[:, m0:m1, :, :], src[:, m0:m1, :, :])
-            elif kind == "qw":
-                e = a[0]
-                nc.vector.quantize_mx(out=w1c[e][:].bitcast(FP8X4), scales=w1s[e][:], in_=w1b[e][:])
-            elif kind == "mm1":
-                e, half = a
-                g = 0 if e < 2 else e
-                c0 = e * C - span[g][0] + half * HALF
-                banks[(e, half)] = psum1.tile([P, PACK, HALF], F32, name="bank")
-                for t in range(PACK):
-                    chans = slice(t * P, (t + 1) * P)
-                    nc.tensor.matmul_mx(
-                        out=banks[(e, half)][:, t, :],
-                        lhsT=w1c[e][:, chans].bitcast(FP8X4),
-                        lhsT_scale=w1s[e][:, chans],
-                        rhs=xc[g][:, c0 : c0 + HALF].bitcast(FP8X4),
-                        rhs_scale=xs[g][:, c0 : c0 + HALF],
-                        start=True,
-                        stop=True,
-                    )
-            elif kind == "si":
-                e, half = a
-                if "hb" not in late:
-                    late["hb"] = keep.tile([P, E * C, PACK], BF16, name="hb", tag="slot_a", align_bytes=64)
-                nc.scalar.activation(
-                    out=late["hb"][:, e * C + half * HALF : e * C + (half + 1) * HALF, :],
-                    in_=banks[(e, half)][:].rearrange("p t n -> p n t"),
-                    func=SILU,
-                )
-            elif kind == "qh":
-                e = a[0]
-                if "hs" not in late:
-                    late["hs"] = keep.tile([P, E * C], U8, name="hs", tag="slot_b", align_bytes=64)
-                slots = slice(e * C, (e + 1) * C)
-                nc.vector.quantize_mx(
-                    out=hc[:, slots].bitcast(FP8X4),
-                    scales=late["hs"][:, slots],
-                    in_=late["hb"][:, slots, :].rearrange("p n t -> p (n t)"),
-                )
-            elif kind == "w2i":
-                engine, e0, e1 = W2_PARTS[a[0]]
-                move(nc, engine, w2b[:, e0:e1, :, :], w2_raw[:, e0:e1, :, :].rearrange("p e j n -> p e n j"))
-            elif kind == "qw2":
-                nc.vector.quantize_mx(
-                    out=w2c[:].bitcast(FP8X4), scales=w2s[:], in_=w2b[:].rearrange("p e n j -> p (e n j)")
-                )
-            elif kind == "mm2":
-                e = a[0]
-                accs[e] = psum2.tile([P, C], F32, name="acc")
-                feats = slice(e * N, (e + 1) * N)
+        w1b = keep.tile([P, E * PACK * H], BF16, name="w1b", align_bytes=64)
+        w1c = keep.tile([P, E * H], U32, name="w1c", align_bytes=64)
+        w1s = keep.tile([P, E * H], U8, name="w1s", align_bytes=64)
+
+        def w1_interleave(e):
+            dst = w1b[:, e * PACK * H : (e + 1) * PACK * H].rearrange("p (t m j) -> p m t j", t=PACK, j=PACK)
+            src = w1_raw[e][:].rearrange("p j (m t) -> p m t j", t=PACK)
+            for engine, m0, m1 in W1_PARTS[e]:
+                if engine == "s":
+                    nc.scalar.copy(out=dst[:, m0:m1, :, :], in_=src[:, m0:m1, :, :])
+                elif engine == "v":
+                    nc.vector.tensor_copy(out=dst[:, m0:m1, :, :], in_=src[:, m0:m1, :, :])
+                else:
+                    nc.gpsimd.tensor_scalar(dst[:, m0:m1, :, :], src[:, m0:m1, :, :], 1.0, 0.0, MULT, ADD)
+
+        def w1_quantize(e0, e1):
+            nc.vector.quantize_mx(
+                out=w1c[:, e0 * H : e1 * H].bitcast(FP8X4),
+                scales=w1s[:, e0 * H : e1 * H],
+                in_=w1b[:, e0 * PACK * H : e1 * PACK * H],
+            )
+
+        w1_interleave(0)
+        w1_interleave(1)
+        w1_quantize(0, 2)
+        w1_interleave(2)
+        w1_quantize(2, 3)
+        w1_interleave(3)
+        w1_quantize(3, 4)
+
+        banks = {}
+
+        def layer1(e, half):
+            bank = psum1.tile([P, PACK, HALF], F32, name="bank")
+            slots = slice(e * C + half * HALF, e * C + (half + 1) * HALF)
+            for t in range(PACK):
+                chans = slice(e * H + t * P, e * H + (t + 1) * P)
                 nc.tensor.matmul_mx(
-                    out=accs[e][:],
-                    lhsT=w2c[:, feats].bitcast(FP8X4),
-                    lhsT_scale=w2s[:, feats],
-                    rhs=hc[:, e * C : (e + 1) * C].bitcast(FP8X4),
-                    rhs_scale=late["hs"][:, e * C : (e + 1) * C],
+                    out=bank[:, t, :],
+                    lhsT=w1c[:, chans].bitcast(FP8X4),
+                    lhsT_scale=w1s[:, chans],
+                    rhs=xc[:, slots].bitcast(FP8X4),
+                    rhs_scale=xs[:, slots],
                     start=True,
                     stop=True,
                 )
-            elif kind == "yc":
-                e = a[0]
-                nc.scalar.copy(out=y[e][:], in_=accs[e][:])
-            else:
-                e = a[0]
-                nc.vector.tensor_tensor(
-                    window[:].indirect(offsets[:, e * C // 16 : (e + 1) * C // 16]),
-                    y[e][:],
-                    gate_sb[:, e * C : (e + 1) * C],
-                    MULT,
+            banks[(e, half)] = bank
+
+        for e in range(E - 1):
+            layer1(e, 0)
+            layer1(e, 1)
+
+        hb = keep.tile([P, E * C, PACK], BF16, name="hb", tag="slot_a", align_bytes=64)
+        hc = keep.tile([P, E * C], U32, name="hc", align_bytes=64)
+
+        def silu(e):
+            for half in range(C // HALF):
+                slots = slice(e * C + half * HALF, e * C + (half + 1) * HALF)
+                nc.scalar.activation(out=hb[:, slots, :], in_=banks[(e, half)][:].rearrange("p t n -> p n t"), func=SILU)
+
+        silu(0)
+        silu(1)
+
+        w2b = keep.tile([P, E, N, PACK], BF16, name="w2b", tag="slot_b", align_bytes=64)
+        w2c = keep.tile([P, E * N], U32, name="w2c", align_bytes=64)
+        w2s = keep.tile([P, E * N], U8, name="w2s", align_bytes=64)
+        nc.vector.tensor_copy(out=w2b[:], in_=w2_raw[:].rearrange("p e j n -> p e n j"))
+        nc.vector.quantize_mx(out=w2c[:].bitcast(FP8X4), scales=w2s[:], in_=w2b[:].rearrange("p e n j -> p (e n j)"))
+        hs = keep.tile([P, E * C], U8, name="hs", tag="slot_b", align_bytes=64)
+
+        def h_quantize(e0, e1):
+            slots = slice(e0 * C, e1 * C)
+            nc.vector.quantize_mx(
+                out=hc[:, slots].bitcast(FP8X4), scales=hs[:, slots], in_=hb[:, slots, :].rearrange("p n t -> p (n t)")
+            )
+
+        window = keep.tile([P, T], F32, name="window")
+        ys = {}
+
+        def layer2(pair):
+            acc = psum2.tile([P, 2, C], F32, name="acc")
+            for i in range(2):
+                e = 2 * pair + i
+                nc.tensor.matmul_mx(
+                    out=acc[:, i, :],
+                    lhsT=w2c[:, e * N : (e + 1) * N].bitcast(FP8X4),
+                    lhsT_scale=w2s[:, e * N : (e + 1) * N],
+                    rhs=hc[:, e * C : (e + 1) * C].bitcast(FP8X4),
+                    rhs_scale=hs[:, e * C : (e + 1) * C],
+                    start=True,
+                    stop=True,
                 )
+            y = keep.tile([P, 2 * C], F32, name="y%d" % pair)
+            nc.scalar.copy(out=y[:], in_=acc[:].rearrange("p i c -> p (i c)"))
+            ys[pair] = y
+
+        def scatter(pair):
+            slots = slice(2 * pair * C, 2 * (pair + 1) * C)
+            cols = slice(2 * pair * C // 16, 2 * (pair + 1) * C // 16)
+            nc.vector.tensor_tensor(window[:].indirect(offsets[:, cols]), ys[pair][:], gate_sb[:, slots], MULT)
+
+        h_quantize(0, 2)
+        layer1(E - 1, 0)
+        layer1(E - 1, 1)
+        layer2(0)
+        silu(2)
+        h_quantize(2, 3)
+        silu(3)
+        h_quantize(3, 4)
+        layer2(1)
+        scatter(0)
+        scatter(1)
 
         nc.sync.dma_start(out, window[:])

@@ -19,9 +19,11 @@ COPY = mybir.ActivationFunctionType.Copy
 P = 128
 PACK = 4
 HALF = 128
-V_SLOTS = 3 * C
+CUT = 512
+PLANE_ORDER = (2, 3, 0, 1)
+S_PLANES = (2, 3)
 W1_PARTS = (
-    (("g", 0, 32), ("v", 32, 128)),
+    (("g", 0, 32), ("s", 32, 128)),
     (("s", 0, 64), ("g", 64, 128)),
     (("s", 0, 64), ("g", 64, 128)),
     (("s", 0, 96), ("g", 96, 128)),
@@ -40,7 +42,7 @@ def tile_routed_moe_kernel(tc, xT, w1, w2, gate, offs, out):
         nc.sync.dma_start(offsets[:], offs)
         x_view = xT.rearrange("(p t) n -> p t n", t=PACK)
         x_raw = keep.tile([P, PACK, T], F32, name="x_raw")
-        for t in range(PACK):
+        for t in PLANE_ORDER:
             nc.sync.dma_start(x_raw[:, t, :], x_view[:, t, :])
         w1_raw = [
             keep.tile([P, PACK, H], F32, name="w1raw%d" % e, tag=("slot_a" if e == E - 1 else "w1raw%d" % e), align_bytes=64)
@@ -60,18 +62,21 @@ def tile_routed_moe_kernel(tc, xT, w1, w2, gate, offs, out):
         nc.vector.memset(warm_in[:], 0.0)
         nc.scalar.activation(out=warm_out[:], in_=warm_in[:], func=SILU)
 
-        x_bf = keep.tile([P, PACK, T], BF16, name="x_bf")
+        x_bf = keep.tile([P, 2, T], BF16, name="x_bf")
         xb = keep.tile([P, E * C, PACK], BF16, name="xb", align_bytes=64)
         xc = keep.tile([P, E * C], U32, name="xc", align_bytes=64)
         xs = keep.tile([P, E * C], U8, name="xs", align_bytes=64)
-        for t in range(PACK):
-            nc.scalar.copy(out=x_bf[:, t, :], in_=x_raw[:, t, :])
-        for t in range(PACK):
-            nc.vector.tensor_copy(xb[:, 0:V_SLOTS, t], x_raw[:, t, :].indirect(offsets[:, 0 : V_SLOTS // 16]))
-        for t in range(PACK):
+        for t in S_PLANES:
+            nc.scalar.copy(out=x_bf[:, t - 2, :], in_=x_raw[:, t, :])
+        for t in PLANE_ORDER:
+            for s0 in range(0, CUT if t in S_PLANES else E * C, CUT):
+                nc.vector.tensor_copy(
+                    xb[:, s0 : s0 + CUT, t], x_raw[:, t, :].indirect(offsets[:, s0 // 16 : (s0 + CUT) // 16])
+                )
+        for t in S_PLANES:
             nc.scalar.activation(
-                out=xb[:, V_SLOTS : E * C, t],
-                in_=x_bf[:, t, :].indirect(offsets[:, V_SLOTS // 16 : E * C // 16]),
+                out=xb[:, CUT : E * C, t],
+                in_=x_bf[:, t - 2, :].indirect(offsets[:, CUT // 16 : E * C // 16]),
                 func=COPY,
             )
         nc.vector.quantize_mx(out=xc[:].bitcast(FP8X4), scales=xs[:], in_=xb[:].rearrange("p n t -> p (n t)"))

@@ -24,8 +24,8 @@ PLANE_ORDER = (2, 3, 0, 1)
 S_PLANES = (2, 3)
 W1_PARTS = (
     (("g", 0, 32), ("s", 32, 128)),
-    (("s", 0, 64), ("g", 64, 128)),
-    (("s", 0, 64), ("g", 64, 128)),
+    (("s", 0, 96), ("g", 96, 128)),
+    (("s", 0, 96), ("g", 96, 128)),
     (("s", 0, 96), ("g", 96, 128)),
 )
 

@@ -86,8 +86,8 @@ def tile_routed_moe_kernel(tc, xT, w1, w2, gate, offs, out):
         w1s = keep.tile([P, E * H], U8, name="w1s", align_bytes=64)
 
         def w1_interleave(e):
-            dst = w1b[:, e * PACK * H : (e + 1) * PACK * H].rearrange("p (t m j) -> p m t j", t=PACK, j=PACK)
-            src = w1_raw[e][:].rearrange("p j (m t) -> p m t j", t=PACK)
+            dst = w1b[:, e * PACK * H : (e + 1) * PACK * H].rearrange("p (t m j) -> p m j t", t=PACK, j=PACK)
+            src = w1_raw[e][:].rearrange("p j (m t) -> p m j t", t=PACK)
             for engine, m0, m1 in W1_PARTS[e]:
                 if engine == "s":
                     nc.scalar.copy(out=dst[:, m0:m1, :, :], in_=src[:, m0:m1, :, :])
@@ -147,7 +147,9 @@ def tile_routed_moe_kernel(tc, xT, w1, w2, gate, offs, out):
         w2b = keep.tile([P, E, N, PACK], BF16, name="w2b", tag="slot_b", align_bytes=64)
         w2c = keep.tile([P, E * N], U32, name="w2c", align_bytes=64)
         w2s = keep.tile([P, E * N], U8, name="w2s", align_bytes=64)
-        nc.vector.tensor_copy(out=w2b[:], in_=w2_raw[:].rearrange("p e j n -> p e n j"))
+        nc.vector.tensor_copy(
+            out=w2b[:].rearrange("p e (c i) j -> p e c j i", i=PACK), in_=w2_raw[:].rearrange("p e j (c i) -> p e c j i", i=PACK)
+        )
         nc.vector.quantize_mx(out=w2c[:].bitcast(FP8X4), scales=w2s[:], in_=w2b[:].rearrange("p e n j -> p (e n j)"))
         hs = keep.tile([P, E * C], U8, name="hs", tag="slot_b", align_bytes=64)
 

@@ -20,7 +20,7 @@ P = 128
 PACK = 4
 HALF = 128
 CUT = 512
-PLANE_ORDER = (2, 3, 0, 1)
+PLANE_ORDER = (2, 3, 1, 0)
 S_PLANES = (2, 3)
 W1_PARTS = (
     (("g", 0, 32), ("s", 32, 128)),
@@ -68,11 +68,12 @@ def tile_routed_moe_kernel(tc, xT, w1, w2, gate, offs, out):
         xs = keep.tile([P, E * C], U8, name="xs", align_bytes=64)
         for t in S_PLANES:
             nc.scalar.copy(out=x_bf[:, t - 2, :], in_=x_raw[:, t, :])
+        x_flat = x_raw[:].rearrange("p t n -> p (t n)")
         for t in PLANE_ORDER:
-            for s0 in range(0, CUT if t in S_PLANES else E * C, CUT):
-                nc.vector.tensor_copy(
-                    xb[:, s0 : s0 + CUT, t], x_raw[:, t, :].indirect(offsets[:, s0 // 16 : (s0 + CUT) // 16])
-                )
+            if t in S_PLANES:
+                nc.vector.tensor_copy(xb[:, 0:CUT, t], x_raw[:, t, :].indirect(offsets[:, 0 : CUT // 16]))
+            else:
+                nc.vector.tensor_copy(xb[:, :, t], x_flat[:, t * T : (t + 2) * T].indirect(offsets[:]))
         for t in S_PLANES:
             nc.scalar.activation(
                 out=xb[:, CUT : E * C, t],

@@ -19,7 +19,7 @@ COPY = mybir.ActivationFunctionType.Copy
 P = 128
 PACK = 4
 HALF = 128
-CUT = 512
+CUT = 384
 PLANE_ORDER = (2, 3, 1, 0)
 S_PLANES = (2, 3)
 W1_PARTS = (

@@ -19,7 +19,7 @@ COPY = mybir.ActivationFunctionType.Copy
 P = 128
 PACK = 4
 HALF = 128
-CUT = 384
+CUT = 256
 PLANE_ORDER = (2, 3, 1, 0)
 S_PLANES = (2, 3)
 W1_PARTS = (

@@ -66,8 +66,8 @@ def tile_routed_moe_kernel(tc, xT, w1, w2, gate, offs, out):
         xb = keep.tile([P, E * C, PACK], BF16, name="xb", align_bytes=64)
         xc = keep.tile([P, E * C], U32, name="xc", align_bytes=64)
         xs = keep.tile([P, E * C], U8, name="xs", align_bytes=64)
-        for t in S_PLANES:
-            nc.scalar.copy(out=x_bf[:, t - 2, :], in_=x_raw[:, t, :])
+        nc.scalar.copy(out=x_bf[:, 0, :], in_=x_raw[:, 2, :])
+        nc.gpsimd.tensor_scalar(x_bf[:, 1, :], x_raw[:, 3, :], 1.0, 0.0, MULT, ADD)
         x_flat = x_raw[:].rearrange("p t n -> p (t n)")
         for t in PLANE_ORDER:
             if t in S_PLANES:

from contextlib import ExitStack

import concourse.mybir as mybir

K, T, E, C, H, N = 512, 1024, 4, 256, 512, 128
FLOPS = 2 * E * C * (K * H + H * N)

F32 = mybir.dt.float32
BF16 = mybir.dt.bfloat16
U32 = mybir.dt.uint32
U16 = mybir.dt.uint16
U8 = mybir.dt.uint8
FP8X4 = mybir.dt.float8_e4m3fn_x4
MULT = mybir.AluOpType.mult
ADD = mybir.AluOpType.add
SILU = mybir.ActivationFunctionType.Silu
COPY = mybir.ActivationFunctionType.Copy

P = 128
PACK = 4
HALF = 128
CUT = 256
PLANE_ORDER = (2, 3, 1, 0)
S_PLANES = (2, 3)
W1_PARTS = (
    (("g", 0, 32), ("s", 32, 128)),
    (("s", 0, 96), ("g", 96, 128)),
    (("s", 0, 96), ("g", 96, 128)),
    (("s", 0, 96), ("g", 96, 128)),
)


def tile_routed_moe_kernel(tc, xT, w1, w2, gate, offs, out):
    nc = tc.nc
    with ExitStack() as ctx:
        lists = ctx.enter_context(tc.tile_pool(name="lists", bufs=1))
        keep = ctx.enter_context(tc.tile_pool(name="keep", bufs=1))
        psum1 = ctx.enter_context(tc.psum_pool(name="psum1", bufs=6))
        psum2 = ctx.enter_context(tc.psum_pool(name="psum2", bufs=2))

        offsets = lists.tile([P, T // 16], U16, name="offsets")
        nc.sync.dma_start(offsets[:], offs)
        x_view = xT.rearrange("(p t) n -> p t n", t=PACK)
        x_raw = keep.tile([P, PACK, T], F32, name="x_raw")
        for t in PLANE_ORDER:
            nc.sync.dma_start(x_raw[:, t, :], x_view[:, t, :])
        w1_raw = [
            keep.tile([P, PACK, H], F32, name="w1raw%d" % e, tag=("slot_a" if e == E - 1 else "w1raw%d" % e), align_bytes=64)
            for e in range(E)
        ]
        for e in range(E):
            nc.sync.dma_start(w1_raw[e][:], w1[e].rearrange("(p j) c -> p j c", j=PACK))
        w2_raw = keep.tile([P, E, PACK, N], F32, name="w2raw")
        nc.sync.dma_start(
            w2_raw[:].rearrange("p e j n -> p e (j n)"), w2.rearrange("e (p j) n -> p e (j n)", j=PACK)
        )
        gate_sb = keep.tile([P, E * C], F32, name="gate_sb")
        nc.sync.dma_start(gate_sb[:], gate)

        warm_in = keep.tile([P, 1], F32, name="warm_in")
        warm_out = keep.tile([P, 1], F32, name="warm_out")
        nc.vector.memset(warm_in[:], 0.0)
        nc.scalar.activation(out=warm_out[:], in_=warm_in[:], func=SILU)

        x_bf = keep.tile([P, 2, T], BF16, name="x_bf")
        xb = keep.tile([P, E * C, PACK], BF16, name="xb", align_bytes=64)
        xc = keep.tile([P, E * C], U32, name="xc", align_bytes=64)
        xs = keep.tile([P, E * C], U8, name="xs", align_bytes=64)
        nc.scalar.copy(out=x_bf[:, 0, :], in_=x_raw[:, 2, :])
        nc.gpsimd.tensor_scalar(x_bf[:, 1, :], x_raw[:, 3, :], 1.0, 0.0, MULT, ADD)
        x_flat = x_raw[:].rearrange("p t n -> p (t n)")
        for t in PLANE_ORDER:
            if t in S_PLANES:
                nc.vector.tensor_copy(xb[:, 0:CUT, t], x_raw[:, t, :].indirect(offsets[:, 0 : CUT // 16]))
            else:
                nc.vector.tensor_copy(xb[:, :, t], x_flat[:, t * T : (t + 2) * T].indirect(offsets[:]))
        for t in S_PLANES:
            nc.scalar.activation(
                out=xb[:, CUT : E * C, t],
                in_=x_bf[:, t - 2, :].indirect(offsets[:, CUT // 16 : E * C // 16]),
                func=COPY,
            )
        nc.vector.quantize_mx(out=xc[:].bitcast(FP8X4), scales=xs[:], in_=xb[:].rearrange("p n t -> p (n t)"))

        w1b = keep.tile([P, E * PACK * H], BF16, name="w1b", align_bytes=64)
        w1c = keep.tile([P, E * H], U32, name="w1c", align_bytes=64)
        w1s = keep.tile([P, E * H], U8, name="w1s", align_bytes=64)

        def w1_interleave(e):
            dst = w1b[:, e * PACK * H : (e + 1) * PACK * H].rearrange("p (t m j) -> p m j t", t=PACK, j=PACK)
            src = w1_raw[e][:].rearrange("p j (m t) -> p m j t", t=PACK)
            for engine, m0, m1 in W1_PARTS[e]:
                if engine == "s":
                    nc.scalar.copy(out=dst[:, m0:m1, :, :], in_=src[:, m0:m1, :, :])
                elif engine == "v":
                    nc.vector.tensor_copy(out=dst[:, m0:m1, :, :], in_=src[:, m0:m1, :, :])
                else:
                    nc.gpsimd.tensor_scalar(dst[:, m0:m1, :, :], src[:, m0:m1, :, :], 1.0, 0.0, MULT, ADD)

        def w1_quantize(e0, e1):
            nc.vector.quantize_mx(
                out=w1c[:, e0 * H : e1 * H].bitcast(FP8X4),
                scales=w1s[:, e0 * H : e1 * H],
                in_=w1b[:, e0 * PACK * H : e1 * PACK * H],
            )

        w1_interleave(0)
        w1_interleave(1)
        w1_quantize(0, 2)
        w1_interleave(2)
        w1_quantize(2, 3)
        w1_interleave(3)
        w1_quantize(3, 4)

        banks = {}

        def layer1(e, half):
            bank = psum1.tile([P, PACK, HALF], F32, name="bank")
            slots = slice(e * C + half * HALF, e * C + (half + 1) * HALF)
            for t in range(PACK):
                chans = slice(e * H + t * P, e * H + (t + 1) * P)
                nc.tensor.matmul_mx(
                    out=bank[:, t, :],
                    lhsT=w1c[:, chans].bitcast(FP8X4),
                    lhsT_scale=w1s[:, chans],
                    rhs=xc[:, slots].bitcast(FP8X4),
                    rhs_scale=xs[:, slots],
                    start=True,
                    stop=True,
                )
            banks[(e, half)] = bank

        for e in range(E - 1):
            layer1(e, 0)
            layer1(e, 1)

        hb = keep.tile([P, E * C, PACK], BF16, name="hb", tag="slot_a", align_bytes=64)
        hc = keep.tile([P, E * C], U32, name="hc", align_bytes=64)

        def silu(e):
            for half in range(C // HALF):
                slots = slice(e * C + half * HALF, e * C + (half + 1) * HALF)
                nc.scalar.activation(out=hb[:, slots, :], in_=banks[(e, half)][:].rearrange("p t n -> p n t"), func=SILU)

        silu(0)
        silu(1)

        w2b = keep.tile([P, E, N, PACK], BF16, name="w2b", tag="slot_b", align_bytes=64)
        w2c = keep.tile([P, E * N], U32, name="w2c", align_bytes=64)
        w2s = keep.tile([P, E * N], U8, name="w2s", align_bytes=64)
        nc.vector.tensor_copy(
            out=w2b[:].rearrange("p e (c i) j -> p e c j i", i=PACK), in_=w2_raw[:].rearrange("p e j (c i) -> p e c j i", i=PACK)
        )
        nc.vector.quantize_mx(out=w2c[:].bitcast(FP8X4), scales=w2s[:], in_=w2b[:].rearrange("p e n j -> p (e n j)"))
        hs = keep.tile([P, E * C], U8, name="hs", tag="slot_b", align_bytes=64)

        def h_quantize(e0, e1):
            slots = slice(e0 * C, e1 * C)
            nc.vector.quantize_mx(
                out=hc[:, slots].bitcast(FP8X4), scales=hs[:, slots], in_=hb[:, slots, :].rearrange("p n t -> p (n t)")
            )

        window = keep.tile([P, T], F32, name="window")
        ys = {}

        def layer2(pair):
            acc = psum2.tile([P, 2, C], F32, name="acc")
            for i in range(2):
                e = 2 * pair + i
                nc.tensor.matmul_mx(
                    out=acc[:, i, :],
                    lhsT=w2c[:, e * N : (e + 1) * N].bitcast(FP8X4),
                    lhsT_scale=w2s[:, e * N : (e + 1) * N],
                    rhs=hc[:, e * C : (e + 1) * C].bitcast(FP8X4),
                    rhs_scale=hs[:, e * C : (e + 1) * C],
                    start=True,
                    stop=True,
                )
            y = keep.tile([P, 2 * C], F32, name="y%d" % pair)
            nc.scalar.copy(out=y[:], in_=acc[:].rearrange("p i c -> p (i c)"))
            ys[pair] = y

        def scatter(pair):
            slots = slice(2 * pair * C, 2 * (pair + 1) * C)
            cols = slice(2 * pair * C // 16, 2 * (pair + 1) * C // 16)
            nc.vector.tensor_tensor(window[:].indirect(offsets[:, cols]), ys[pair][:], gate_sb[:, slots], MULT)

        h_quantize(0, 2)
        layer1(E - 1, 0)
        layer1(E - 1, 1)
        layer2(0)
        silu(2)
        h_quantize(2, 3)
        silu(3)
        h_quantize(3, 4)
        layer2(1)
        scatter(0)
        scatter(1)

        nc.sync.dma_start(out, window[:])
